import numpy as np
import ml_dtypes


def mxq(x, axis, fmt="e4m3"):
    dtype, down = {"e4m3": (ml_dtypes.float8_e4m3fn, 7), "e5m2": (ml_dtypes.float8_e5m2, 14)}[fmt]
    v = np.moveaxis(np.asarray(x, np.float32).astype(ml_dtypes.bfloat16).astype(np.float64), axis, -1)
    blocks = v.reshape(v.shape[:-1] + (-1, 32))
    amax = np.abs(blocks).max(-1, keepdims=True)
    byte = np.maximum(np.where(amax > 0, np.frexp(amax)[1] - 1 + 127, 0) - down, 1)
    scale = np.exp2(byte - 127.0)
    codes = (blocks / scale).astype(np.float32).astype(dtype).astype(np.float64)
    return np.moveaxis((codes * scale).reshape(v.shape), -1, axis)


WIDE = False


def mx_kscale(k):
    if not WIDE:
        return np.ones(k)
    levels = np.array([10, -10, 5, -5, 0])
    if k % 512:
        return np.exp2(np.random.permutation(np.resize(levels, k // 32))).repeat(32)
    a = np.empty((k // 512, 16))
    for p in range(k // 512):
        a[p, :8] = np.random.permutation(np.resize(levels, 8))
        for g in range(8):
            far = levels[np.abs(levels - a[p, g]) >= 10]
            a[p, g + 8] = far[np.random.randint(len(far))]
    return np.exp2(a.ravel()).repeat(32)


def f64(x):
    return np.asarray(x).astype(np.float64)


def striped(idx):
    return np.tile(idx.reshape(-1, 16).T, (8, 1)).astype(np.uint16)


def unstriped(offs):
    return offs[:16].T.reshape(-1).astype(np.int64)


E2M1 = np.array([0.0, 0.5, 1.0, 1.5, 2.0, 3.0, 4.0, 6.0, -0.0, -0.5, -1.0, -1.5, -2.0, -3.0, -4.0, -6.0])


def pack_weight(w, fmt):
    k, n = w.shape
    w = f64(np.asarray(w, np.float32).astype(ml_dtypes.bfloat16)).reshape(k // 32, 32, n)
    amax = np.abs(w).max(1)
    if fmt == "e4m3":
        byte = np.frexp(amax)[1] - 1 + 127 - 7
    else:
        mant, ex = np.frexp(amax / 6.0)
        byte = np.where(mant > 0.5, ex, ex - 1) + 127
    byte = np.clip(np.where(amax > 0, byte, 1), 1, 254)
    scaled = (w * np.exp2(127.0 - byte)[:, None, :]).reshape(k, n).astype(np.float32)
    by_word = np.ascontiguousarray(scaled.reshape(k // 512, 128, 4, n).transpose(0, 1, 3, 2))
    if fmt == "e4m3":
        words = by_word.astype(ml_dtypes.float8_e4m3fn).view(np.uint8)
    else:
        c = by_word.astype(ml_dtypes.float4_e2m1fn).view(np.uint8) & 0xF
        words = (c[..., 0::2] | (c[..., 1::2] << 4)).reshape(k // 512, 128, 2 * n)
    return np.ascontiguousarray(words), np.ascontiguousarray(byte.astype(np.uint8).reshape(k // 512, 16, n))


def unpack_weight(words, scales, fmt):
    g, _, n = scales.shape
    words = np.ascontiguousarray(words).reshape(g, 128, n, -1)
    if fmt == "e4m3":
        vals = words.view(ml_dtypes.float8_e4m3fn).astype(np.float64)
    else:
        nib = np.empty((g, 128, n, 4), np.uint8)
        nib[..., 0::2] = words & 0xF
        nib[..., 1::2] = words >> 4
        vals = E2M1[nib]
    vals = vals * np.repeat(np.exp2(scales.astype(np.float64) - 127.0), 8, axis=1)[..., None]
    return vals.transpose(0, 1, 3, 2).reshape(g * 512, n)


def gelu(v):
    return 0.5 * v * (1.0 + np.tanh(np.sqrt(2.0 / np.pi) * (v + 0.044715 * v**3)))


K, H, N, T, S, P, P2 = 1024, 1536, 768, 4096, 1024, 512, 256

def setup_inputs():
    n = np.random.standard_normal
    s = mx_kscale(K)[:, None]
    u = mx_kscale(H)[:, None]
    tab_words, tab_scales = pack_weight(n((K, T)) * s, "e4m3")
    w4_words, w4_scales = pack_weight(n((H, N)) * 0.8 / np.sqrt(H) / u, "e2m1")
    return {
        "tab_words": tab_words, "tab_scales": tab_scales,
        "offs": striped(np.random.permutation(T)[:S]),
        "w1": (n((K, H)) * 1.5 / np.sqrt(K) / s).astype(np.float32),
        "gain": (np.exp(0.3 * n(H)) * np.sqrt(u[:, 0])).astype(np.float32),
        "pos1": striped(np.random.permutation(S)[:P]),
        "pos2": striped(np.random.permutation(S)[:P]),
        "salt": (0.8 * n((H, P)) * u).astype(np.float32),
        "w4_words": w4_words, "w4_scales": w4_scales,
        "pos3": striped(np.random.permutation(P)[:P2]),
        "pos4": striped(np.random.permutation(P)[:P2]),
    }

def reference(tab_words, tab_scales, offs, w1, gain, pos1, pos2, salt, w4_words, w4_scales, pos3, pos4):
    v = unpack_weight(tab_words, tab_scales, "e4m3")[:, unstriped(offs)]
    w4 = unpack_weight(w4_words, w4_scales, "e2m1")
    a = mxq(f64(w1), 0, "e4m3").T @ v
    h = a / (1.0 + np.exp(-a)) * f64(gain)[:, None]
    z = h[:, unstriped(pos1)] * h[:, unstriped(pos2)] + f64(salt)
    y = np.tanh(w4.T @ mxq(z, 0, "e4m3"))
    return np.maximum(y[:, unstriped(pos3)], y[:, unstriped(pos4)])

from contextlib import ExitStack

import concourse.mybir as mybir

K, H, N, T, S, P1, P2 = 1024, 1536, 768, 4096, 1024, 512, 256
FLOPS = 2 * K * H * S + 2 * H * N * P1

F32 = mybir.dt.float32
BF16 = mybir.dt.bfloat16
I32 = mybir.dt.int32
U32 = mybir.dt.uint32
U16 = mybir.dt.uint16
U8 = mybir.dt.uint8
FP8X4 = mybir.dt.float8_e4m3fn_x4
FP4X4 = mybir.dt.float4_e2m1fn_x4
ACT = mybir.ActivationFunctionType
ALU = mybir.AluOpType

P = 128
PASS = 512
A1 = K // PASS
B2 = H // PASS
HALF = 512
NT = N // P


def tile_list_ham_probing_round_kernel(
    tc, tab_words, tab_scales, offs, w1, gain, pos1, pos2, salt, w4_words, w4_scales, pos3, pos4, out
):
    nc = tc.nc
    with ExitStack() as ctx:
        keep = ctx.enter_context(tc.tile_pool(name="keep", bufs=1))
        ring = ctx.enter_context(tc.tile_pool(name="ring", bufs=2))
        psum = ctx.enter_context(tc.psum_pool(name="psum", bufs=1))

        offs_t = keep.tile([P, S // 16], U16, name="offs_t")
        pos1_t = keep.tile([P, P1 // 16], U16, name="pos1_t")
        pos2_t = keep.tile([P, P1 // 16], U16, name="pos2_t")
        pos3_t = keep.tile([P, P2 // 16], U16, name="pos3_t")
        pos4_t = keep.tile([P, P2 // 16], U16, name="pos4_t")

        tabw = [keep.tile([P, T], U32, name="tabw%d" % a, align_bytes=64) for a in range(A1)]
        tabs = keep.tile([P, T], U8, name="tabs", tag="tabs", align_bytes=64)
        w4w = keep.tile([P, B2, 2 * N], U8, name="w4w", align_bytes=64)
        w4s = keep.tile([P, B2, N], U8, name="w4s", align_bytes=64)
        gain_t = keep.tile([P, B2, 4], F32, name="gain_t")
        gain2 = keep.tile([P, B2, 4], F32, name="gain2")
        salt_t = [keep.tile([P, 4, P1], F32, name="salt%d" % b) for b in range(B2)]
        vw = {}
        vs = [keep.tile([P, HALF], U8, name="vs%d" % hf, align_bytes=64) for hf in range(2)]
        wc = {}
        ws = {}
        for b in range(B2):
            for a in range(A1):
                wc[a, b] = keep.tile([P, PASS], U32, name="wc%d%d" % (a, b), align_bytes=64)
                ws[a, b] = keep.tile([P, PASS], U8, name="ws%d%d" % (a, b), align_bytes=64)
        zc = [keep.tile([P, P1], U32, name="zc%d" % b, align_bytes=64) for b in range(B2)]
        zs = [keep.tile([P, P1], U8, name="zs%d" % b, align_bytes=64) for b in range(B2)]

        raw = {}

        def load_w1(a, b):
            raw[a, b] = ring.tile([P, 4, PASS], F32, name="raw", tag="raw", bufs=4)
            nc.sync.dma_start(
                out=raw[a, b][:],
                in_=w1[PASS * a : PASS * (a + 1), PASS * b : PASS * (b + 1)].rearrange("(p j) c -> p j c", j=4),
            )

        def load_tab(a):
            nc.sync.dma_start(
                out=tabw[a][:].bitcast(I32), in_=tab_words[a].rearrange("p t i -> p (t i)").bitcast(I32)
            )

        def load_salt(b):
            nc.sync.dma_start(
                out=salt_t[b][:], in_=salt[PASS * b : PASS * (b + 1), :].rearrange("(p t) m -> p t m", t=4)
            )

        nc.vector.memset(tabs[:].bitcast(I32), 0)
        nc.vector.memset(w4s[:].rearrange("p b n -> p (b n)").bitcast(I32), 0)
        nc.sync.dma_start(offs_t[:], offs)
        load_tab(0)
        for q in range(4):
            nc.gpsimd.dma_start(
                out=tabs[32 * q : 32 * q + 8, :].bitcast(I32),
                in_=tab_scales[:, 4 * q : 4 * q + 4, :].bitcast(I32),
            )
        load_w1(0, 0)
        load_tab(1)
        load_w1(1, 0)
        nc.sync.dma_start(pos1_t[:], pos1)
        nc.sync.dma_start(pos2_t[:], pos2)
        nc.sync.dma_start(out=gain_t[:], in_=gain.rearrange("(b p t) -> p b t", p=P, t=4))
        load_salt(0)
        for b in range(1, B2):
            load_w1(0, b)
            load_w1(1, b)
            load_salt(b)
        nc.sync.dma_start(out=w4w[:].bitcast(I32), in_=w4_words.rearrange("a p c -> p a c").bitcast(I32))
        for q in range(4):
            nc.sync.dma_start(
                out=w4s[32 * q : 32 * q + 4, :, :].bitcast(I32),
                in_=w4_scales[:, 4 * q : 4 * q + 4, :].rearrange("a r n -> r a n").bitcast(I32),
            )
        nc.sync.dma_start(pos3_t[:], pos3)
        nc.sync.dma_start(pos4_t[:], pos4)

        nc.vector.tensor_tensor(out=gain2[:], in0=gain_t[:], in1=gain_t[:], op=ALU.mult)

        def gather_words(a):
            for hf in range(2):
                tag = "tabs" if (a, hf) == (1, 0) else "vw%d%d" % (a, hf)
                vw[a, hf] = keep.tile([P, HALF], U32, name="vw", tag=tag, align_bytes=64)
                nc.vector.tensor_copy(out=vw[a, hf][:], in_=tabw[a][:].indirect(offs_t[:, 32 * hf : 32 * (hf + 1)]))

        def gather_scales():
            for hf in range(2):
                nc.vector.tensor_copy(out=vs[hf][:], in_=tabs[:].indirect(offs_t[:, 32 * hf : 32 * (hf + 1)]))

        def quantize_w1(a, b, vector_share):
            wg = keep.tile([P, 4, P, 4], BF16, name="wg", tag="wg%d%d" % (a, b), align_bytes=64)
            dst = wg[:].rearrange("p t m j -> p m j t")
            src = raw[a, b][:].rearrange("p j (m t) -> p m j t", t=4)
            if vector_share:
                nc.vector.tensor_copy(out=dst[:, :vector_share], in_=src[:, :vector_share])
            nc.scalar.copy(out=dst[:, vector_share:], in_=src[:, vector_share:])
            flat = wg[:].rearrange("p t m j -> p (t m j)")
            cuts = [0, P, PASS] if vector_share else [0, PASS]
            for c0, c1 in zip(cuts[:-1], cuts[1:]):
                nc.vector.quantize_mx(
                    out=wc[a, b][:, c0:c1].bitcast(FP8X4), scales=ws[a, b][:, c0:c1], in_=flat[:, 4 * c0 : 4 * c1]
                )

        def stage1(b, t, zb):
            i = 4 * b + t
            if i in (4, 8):
                h = keep.tile([P, S], F32, name="h", tag="hz%d" % (b - 1), align_bytes=64)
            else:
                h = ring.tile([P, S], F32, name="h", tag="h", bufs=4)
            for hf in range(2):
                acc = psum.tile([P, HALF], F32, name="acc", tag="acc", bufs=2)
                for a in range(A1):
                    nc.tensor.matmul_mx(
                        out=acc[:],
                        lhsT=wc[a, b][:, P * t : P * (t + 1)].bitcast(FP8X4),
                        lhsT_scale=ws[a, b][:, P * t : P * (t + 1)],
                        rhs=vw[a, hf][:].bitcast(FP8X4),
                        rhs_scale=vs[hf][4 * a : P, :],
                        start=(a == 0),
                        stop=(a == A1 - 1),
                    )
                nc.scalar.activation(out=h[:, HALF * hf : HALF * (hf + 1)], in_=acc[:], func=ACT.Silu)
            if i in (3, 6):
                first = keep.tile([P, P1], F32, name="first", tag="wg1%d" % (b + 1), align_bytes=64)
            else:
                first = ring.tile([P, P1], F32, name="first", tag="first", bufs=2)
            prod = ring.tile([P, P1], F32, name="prod", tag="prod", bufs=2)
            halves = [(slice(256 * u, 256 * (u + 1)), slice(16 * u, 16 * (u + 1))) for u in range(2)]
            for cols, lst in halves:
                nc.vector.tensor_copy(out=first[:, cols], in_=h[:].indirect(pos1_t[:, lst]))
            for cols, lst in halves:
                nc.vector.tensor_tensor(
                    out=prod[:, cols], in0=h[:].indirect(pos2_t[:, lst]), in1=first[:, cols], op=ALU.mult
                )
            for cols, lst in halves:
                nc.vector.scalar_tensor_tensor(
                    out=zb[:, t, cols], in0=prod[:, cols], scalar=gain2[:, b, t : t + 1], in1=salt_t[b][:, t, cols],
                    op0=ALU.mult, op1=ALU.add,
                )

        ybank = [psum.tile([P, P1], F32, name="ybank%d" % n) for n in range(NT)]

        def stage2(b, zb, vector_share):
            zi = keep.tile([P, P1, 4], BF16, name="zi", tag="hz%d" % b, align_bytes=64)
            dst = zi[:].rearrange("p (c i) t -> p c t i", i=4)
            src = zb[:].rearrange("p t (c i) -> p c t i", i=4)
            if vector_share:
                nc.vector.tensor_copy(out=dst[:, :vector_share], in_=src[:, :vector_share])
            nc.scalar.copy(out=dst[:, vector_share:], in_=src[:, vector_share:])
            nc.vector.quantize_mx(
                out=zc[b][:].bitcast(FP8X4), scales=zs[b][:], in_=zi[:].rearrange("p m t -> p (m t)")
            )
            for n in range(NT):
                nc.tensor.matmul_mx(
                    out=ybank[n][:],
                    lhsT=w4w[:, b, 2 * P * n : 2 * P * (n + 1)].bitcast(FP4X4),
                    lhsT_scale=w4s[:, b, P * n : P * (n + 1)],
                    rhs=zc[b][:].bitcast(FP8X4),
                    rhs_scale=zs[b][:],
                    start=(b == 0),
                    stop=(b == B2 - 1),
                )

        gather_words(0)
        quantize_w1(0, 0, 0)
        gather_scales()
        gather_words(1)
        quantize_w1(1, 0, 84)
        zbs = [keep.tile([P, 4, P1], BF16, name="zb%d" % b) for b in range(B2)]
        for b in range(B2):
            for t in range(4):
                stage1(b, t, zbs[b])
                if b + 1 < B2 and t in (0, 1):
                    quantize_w1(t, b + 1, 0)
                if b > 0 and t == 1:
                    stage2(b - 1, zbs[b - 1], 0)
        stage2(B2 - 1, zbs[B2 - 1], 84)

        picked = {}

        def finish(n):
            res = ring.tile([P, P2], F32, name="res", tag="res", bufs=3)
            nc.vector.tensor_tensor(out=res[:], in0=picked[n][0][:], in1=picked[n][1][:], op=ALU.max)
            nc.sync.dma_start(out=out[P * n : P * (n + 1), :], in_=res[:])

        for n in range(NT):
            y = ring.tile([P, P1], F32, name="y", tag="y", bufs=NT)
            nc.scalar.activation(out=y[:], in_=ybank[n][:], func=ACT.Tanh)
            ya = ring.tile([P, P2], F32, name="ya", tag="ya", bufs=2)
            yb = ring.tile([P, P2], F32, name="yb", tag="yb", bufs=2)
            nc.vector.tensor_copy(out=ya[:], in_=y[:].indirect(pos3_t[:]))
            if n > 0:
                finish(n - 1)
            nc.vector.tensor_copy(out=yb[:], in_=y[:].indirect(pos4_t[:]))
            picked[n] = (ya, yb)
        finish(NT - 1)
